import numpy as np
import ml_dtypes


def mxq(x, axis, fmt="e4m3"):
    dtype, down = {"e4m3": (ml_dtypes.float8_e4m3fn, 7), "e5m2": (ml_dtypes.float8_e5m2, 14)}[fmt]
    v = np.moveaxis(np.asarray(x, np.float32).astype(ml_dtypes.bfloat16).astype(np.float64), axis, -1)
    blocks = v.reshape(v.shape[:-1] + (-1, 32))
    amax = np.abs(blocks).max(-1, keepdims=True)
    byte = np.maximum(np.where(amax > 0, np.frexp(amax)[1] - 1 + 127, 0) - down, 1)
    scale = np.exp2(byte - 127.0)
    codes = (blocks / scale).astype(np.float32).astype(dtype).astype(np.float64)
    return np.moveaxis((codes * scale).reshape(v.shape), -1, axis)


WIDE = False


def mx_kscale(k):
    if not WIDE:
        return np.ones(k)
    levels = np.array([10, -10, 5, -5, 0])
    if k % 512:
        return np.exp2(np.random.permutation(np.resize(levels, k // 32))).repeat(32)
    a = np.empty((k // 512, 16))
    for p in range(k // 512):
        a[p, :8] = np.random.permutation(np.resize(levels, 8))
        for g in range(8):
            far = levels[np.abs(levels - a[p, g]) >= 10]
            a[p, g + 8] = far[np.random.randint(len(far))]
    return np.exp2(a.ravel()).repeat(32)


def f64(x):
    return np.asarray(x).astype(np.float64)


def striped(idx):
    return np.tile(idx.reshape(-1, 16).T, (8, 1)).astype(np.uint16)


def unstriped(offs):
    return offs[:16].T.reshape(-1).astype(np.int64)


def pack_weight(w):
    k, n = w.shape
    w = f64(np.asarray(w, np.float32).astype(ml_dtypes.bfloat16)).reshape(k // 32, 32, n)
    amax = np.abs(w).max(1)
    byte = np.clip(np.where(amax > 0, np.frexp(amax)[1] - 1 + 127 - 7, 1), 1, 254)
    scaled = (w * np.exp2(127.0 - byte)[:, None, :]).reshape(k, n).astype(np.float32)
    words = np.ascontiguousarray(scaled.reshape(k // 512, 128, 4, n).transpose(0, 1, 3, 2)).astype(ml_dtypes.float8_e4m3fn).view(np.uint8)
    return words, np.ascontiguousarray(byte.astype(np.uint8).reshape(k // 512, 16, n))


def unpack_weight(words, scales):
    g, p, n, _ = words.shape
    vals = np.ascontiguousarray(words).view(ml_dtypes.float8_e4m3fn).astype(np.float64) * np.repeat(np.exp2(scales.astype(np.float64) - 127.0), 8, axis=1)[..., None]
    return vals.transpose(0, 1, 3, 2).reshape(g * 512, n)

def planes(y):
    n, m = y.shape
    v = y.astype(np.float32).astype(ml_dtypes.bfloat16).astype(np.float64).reshape(n // 32, 32, m)
    top = np.abs(v).max(1)
    byte = np.clip(np.where(top > 0, np.frexp(top)[1] - 1 + 127 - 7, 1), 1, 254)
    codes = (v * np.exp2(127.0 - byte)[:, None, :]).reshape(n, m).astype(np.float32).astype(ml_dtypes.float8_e4m3fn).view(np.uint8)
    words = codes.reshape(n // 512, 128, 4, m).transpose(0, 1, 3, 2)
    return np.ascontiguousarray(words), np.ascontiguousarray(byte.astype(np.uint8).reshape(n // 512, 16, m))


K, T, D, N = 512, 512, 3, 512
P = 2 ** 7


def setup_inputs():
    n = np.random.standard_normal
    s = mx_kscale(K)[:, None]
    packed_xT = pack_weight(n((K, T)) * s)
    return {
        "x_words": packed_xT[0],
        "x_scales": packed_xT[1],
        "w1": (n((K, N)) / np.sqrt(K) / s).astype(np.float32),
        "gate": (np.tile(np.random.uniform(0.2, 1.0, (D, 1, T)) / np.sqrt(D), (1, P, 1))).astype(np.float32),
        "pos1": striped(np.random.permutation(T)),
        "pos2": striped(np.random.permutation(T)),
        "pos3": striped(np.random.permutation(T)),
    }


def reference(x_words, x_scales, w1, gate, pos1, pos2, pos3):
    xq = unpack_weight(x_words, x_scales)
    y = mxq(f64(w1), 0, "e4m3").T @ xq
    out_0 = y + (y[:, unstriped(pos1)] - y) * f64(gate)[0, :1] + (y[:, unstriped(pos2)] - y) * f64(gate)[1, :1] + (y[:, unstriped(pos3)] - y) * f64(gate)[2, :1]
    return (out_0,) + planes(out_0)

@@ -1,0 +1,224 @@
+from contextlib import ExitStack
+
+import concourse.mybir as mybir
+from concourse.masks import make_identity
+
+K, N, T, D = 512, 512, 512, 3
+FLOPS = 2 * K * N * T
+
+F32 = mybir.dt.float32
+BF16 = mybir.dt.bfloat16
+I32 = mybir.dt.int32
+U32 = mybir.dt.uint32
+U16 = mybir.dt.uint16
+U8 = mybir.dt.uint8
+FP8X4 = mybir.dt.float8_e4m3fn_x4
+MULT = mybir.AluOpType.mult
+ADD = mybir.AluOpType.add
+COPY = mybir.ActivationFunctionType.Copy
+
+P = 128
+PACK = 4
+HALF = T // 2
+BLOCKS = T // P
+W_SPLIT = 40
+
+
+def tile_picked_wgrand_none_lo_kernel(
+    tc, x_words, x_scales, w1, gate, pos1, pos2, pos3, out_0, out_1, out_2
+):
+    nc = tc.nc
+    with ExitStack() as ctx:
+        keep = ctx.enter_context(tc.tile_pool(name="keep", bufs=1))
+        psum = ctx.enter_context(tc.psum_pool(name="psum", bufs=1))
+
+        def sb(name, shape, dtype):
+            return keep.tile(shape, dtype, name=name, align_bytes=64)
+
+        def bank(i, name):
+            return psum.tile([P, 512], F32, name=name, tag="bank%d" % i)
+
+        lists = [keep.tile([P, T // 16], U16, name="list%d" % d) for d in range(D)]
+        x_scale = sb("x_scale", [P, T], U8)
+        nc.vector.memset(x_scale[:].bitcast(U32), 0)
+        gate_rows = sb("gate_rows", [P, D, P], F32)
+        nc.gpsimd.memset(gate_rows[:], 0.0)
+        ident = sb("ident", [P, P], F32)
+        make_identity(nc, ident[:])
+
+        w_view = w1.rearrange("(p j) m -> p j m", j=PACK)
+        w_raw = [sb("w_raw%d" % h, [P, PACK, N // 2], F32) for h in range(2)]
+        for h in range(2):
+            nc.sync.dma_start(out=w_raw[h][:], in_=w_view[:, :, h * (N // 2) : (h + 1) * (N // 2)])
+        for q in range(4):
+            nc.sync.dma_start(
+                out=x_scale[32 * q : 32 * q + 4, :].bitcast(I32),
+                in_=x_scales[0, 4 * q : 4 * q + 4, :].bitcast(I32),
+            )
+        x_code = sb("x_code", [P, T], U32)
+        nc.sync.dma_start(
+            out=x_code[:].bitcast(I32), in_=x_words[0].rearrange("p c r -> p (c r)").bitcast(I32)
+        )
+        nc.sync.dma_start(
+            out=gate_rows[0:BLOCKS, :, :], in_=gate[:, 0, :].rearrange("d (b v) -> b d v", v=P)
+        )
+        gate_view = gate.rearrange("d p v -> p d v")
+        gates = [sb("gates%d" % h, [P, D, HALF], F32) for h in range(2)]
+        nc.sync.dma_start(lists[0][:], pos1)
+        nc.sync.dma_start(out=gates[0][:], in_=gate_view[:, :, 0:HALF])
+        nc.sync.dma_start(lists[1][:], pos2)
+        nc.sync.dma_start(lists[2][:], pos3)
+        nc.sync.dma_start(out=gates[1][:], in_=gate_view[:, :, HALF:T])
+
+        w_bf = sb("w_bf", [P, PACK, P, PACK], BF16)
+
+        def w_views(h, m0, m1):
+            src = w_raw[h][:, :, PACK * m0 : PACK * m1].rearrange("p j (m t) -> p m t j", t=PACK)
+            dst = w_bf[:, :, 64 * h + m0 : 64 * h + m1, :].rearrange("p t m j -> p m t j")
+            return dst, src
+
+        nc.vector.tensor_copy(*w_views(0, 0, 64))
+        nc.vector.tensor_copy(*w_views(1, 0, W_SPLIT))
+        dst, src = w_views(1, W_SPLIT, 64)
+        nc.scalar.activation(dst, src, COPY)
+
+        w_code = sb("w_code", [P, N], U32)
+        w_scale = sb("w_scale", [P, N], U8)
+        for t0, t1 in ((0, 1), (1, 2), (2, 4)):
+            nc.vector.quantize_mx(
+                out=w_code[:, t0 * P : t1 * P].bitcast(FP8X4),
+                scales=w_scale[:, t0 * P : t1 * P],
+                in_=w_bf[:, t0:t1, :, :].rearrange("p t m j -> p (t m j)"),
+            )
+
+        def project(t, c0, c1, acc):
+            nc.tensor.matmul_mx(
+                out=acc,
+                lhsT=w_code[:, t * P : (t + 1) * P].bitcast(FP8X4),
+                lhsT_scale=w_scale[:, t * P : (t + 1) * P],
+                rhs=x_code[:, c0:c1].bitcast(FP8X4),
+                rhs_scale=x_scale[:, c0:c1],
+                start=True,
+                stop=True,
+            )
+
+        def turn_add(acc, terms):
+            for i, term in enumerate(terms):
+                nc.tensor.matmul(
+                    acc, term, ident[:], start=(i == 0), stop=(i == len(terms) - 1), is_transpose=True
+                )
+
+        y = [sb("y%d" % t, [P, T], F32) for t in range(PACK)]
+        acc_a, acc_b = bank(0, "y0a"), bank(1, "y0b")
+        project(0, 0, HALF, acc_a[:, 0:HALF])
+        project(0, HALF, T, acc_b[:, 0:HALF])
+        nc.scalar.copy(y[0][:, 0:HALF], acc_a[:, 0:HALF])
+        nc.vector.tensor_copy(y[0][:, HALF:T], acc_b[:, 0:HALF])
+        for t in range(1, PACK):
+            acc = bank(1 + t, "y_acc%d" % t)
+            project(t, 0, T, acc[:])
+            nc.scalar.copy(y[t][:], acc[:])
+
+        gate_sum = bank(5, "gate_sum")
+        turn_add(gate_sum[:, 0:P], [gate_rows[:, d, :] for d in range(D)])
+        stay = sb("stay", [P, BLOCKS], F32)
+        nc.scalar.activation(stay[:], gate_sum[:, 0:BLOCKS], COPY, bias=1.0, scale=-1.0)
+
+        own = [sb("own%d" % b, [P, PACK, P], F32) for b in range(BLOCKS)]
+        own_banks = (6, 7, 0, 1)
+
+        def make_own(b):
+            acc = bank(own_banks[b], "own_acc%d" % b)
+            for t in range(PACK):
+                turn_add(acc[:, t * P : (t + 1) * P], [y[t][:, b * P : (b + 1) * P]])
+            nc.scalar.activation(
+                own[b][:].rearrange("v t p -> v (t p)"), acc[:], COPY, scale=stay[:, b : b + 1]
+            )
+
+        def pull(h, t, d):
+            term = sb("term%d_%d_%d" % (h, t, d), [P, HALF], F32)
+            offsets = lists[d][:, h * (HALF // 16) : (h + 1) * (HALF // 16)]
+            nc.vector.tensor_tensor(term[:], y[t][:].indirect(offsets), gates[h][:, d, :], MULT)
+            return term
+
+        def turn_in(h, t, terms):
+            acc = bank(2 + t % 2, "sum_acc%d_%d" % (h, t))
+            for b in range(2):
+                turn_add(acc[:, b * P : (b + 1) * P], [term[:, b * P : (b + 1) * P] for term in terms])
+            turned = sb("turned%d_%d" % (h, t), [P, HALF], F32)
+            nc.scalar.copy(turned[:], acc[:, 0:HALF])
+            return turned
+
+        def turn_back(h, t, turned, i):
+            acc = bank(i, "out_acc%d_%d" % (h, t))
+            for b in range(2):
+                turn_add(
+                    acc[:, b * P : (b + 1) * P],
+                    [own[2 * h + b][:, t, :], turned[:, b * P : (b + 1) * P]],
+                )
+            return acc
+
+        out_view = out_0.rearrange("(p t) v -> p t v", t=PACK)
+        result = [sb("result%d" % h, [P, PACK, HALF], F32) for h in range(2)]
+        out_bf = [sb("out_bf%d" % b, [P, P, PACK], BF16) for b in range(BLOCKS)]
+        out_code = sb("out_code", [P, T], U32)
+        out_scale = sb("out_scale", [P, T], U8)
+        words_view = out_1[0].rearrange("p c r -> p (c r)").bitcast(I32)
+
+        def weave(b, copy):
+            h, c0 = b // 2, (b % 2) * P
+            copy(out_bf[b][:], result[h][:, :, c0 : c0 + P].rearrange("p t v -> p v t"))
+
+        def quantize(b):
+            nc.vector.quantize_mx(
+                out=out_code[:, b * P : (b + 1) * P].bitcast(FP8X4),
+                scales=out_scale[:, b * P : (b + 1) * P],
+                in_=out_bf[b][:].rearrange("p v t -> p (v t)"),
+            )
+
+        make_own(0)
+        make_own(1)
+        turned = {}
+        for t in range(PACK + 1):
+            if t < PACK:
+                turned[t] = turn_in(0, t, [pull(0, t, d) for d in range(D)])
+            if t == 1:
+                make_own(2)
+                make_own(3)
+            if t > 0:
+                acc = turn_back(0, t - 1, turned[t - 1], 4 + (t - 1) % 2)
+                nc.scalar.copy(result[0][:, t - 1, :], acc[:, 0:HALF])
+        nc.sync.dma_start(out=out_view[:, :, 0:HALF], in_=result[0][:])
+
+        partial = {}
+        for t in range(PACK + 1):
+            if t < PACK:
+                turned[t] = turn_in(1, t, [pull(1, t, d) for d in range(D - 1)])
+            if t > 0:
+                partial[t - 1] = turn_back(1, t - 1, turned[t - 1], own_banks[t - 1])
+            if t == 1:
+                weave(0, nc.scalar.copy)
+            if t == 2:
+                weave(1, nc.scalar.copy)
+        quantize(0)
+        quantize(1)
+        nc.sync.dma_start(out=words_view[:, 0:HALF], in_=out_code[:, 0:HALF].bitcast(I32))
+
+        last = {}
+        for t in range(PACK + 1):
+            if t < PACK:
+                last[t] = pull(1, t, D - 1)
+            if t > 0:
+                nc.vector.tensor_tensor(result[1][:, t - 1, :], partial[t - 1][:, 0:HALF], last[t - 1][:], ADD)
+                nc.sync.dma_start(out=out_view[:, t - 1, HALF:T], in_=result[1][:, t - 1, :])
+        weave(2, nc.vector.tensor_copy)
+        weave(3, nc.scalar.copy)
+        quantize(2)
+        quantize(3)
+        nc.sync.dma_start(out=words_view[:, HALF:T], in_=out_code[:, HALF:T].bitcast(I32))
+        for q in range(4):
+            queue = nc.scalar if q % 2 else nc.sync
+            queue.dma_start(
+                out=out_2[0, 4 * q : 4 * q + 4, :].bitcast(I32),
+                in_=out_scale[32 * q : 32 * q + 4, :].bitcast(I32),
+            )

@@ -21,7 +21,6 @@ P = 128
 PACK = 4
 HALF = T // 2
 BLOCKS = T // P
-W_SPLIT = 40
 
 
 def tile_picked_wgrand_none_lo_kernel(
@@ -40,18 +39,19 @@ def tile_picked_wgrand_none_lo_kernel(
 
         lists = [keep.tile([P, T // 16], U16, name="list%d" % d) for d in range(D)]
         x_scale = sb("x_scale", [P, T], U8)
-        nc.vector.memset(x_scale[:].bitcast(U32), 0)
+        nc.gpsimd.memset(x_scale[:].bitcast(U32), 0)
         gate_rows = sb("gate_rows", [P, D, P], F32)
         nc.gpsimd.memset(gate_rows[:], 0.0)
         ident = sb("ident", [P, P], F32)
         make_identity(nc, ident[:])
 
         w_view = w1.rearrange("(p j) m -> p j m", j=PACK)
-        w_raw = [sb("w_raw%d" % h, [P, PACK, N // 2], F32) for h in range(2)]
-        for h in range(2):
-            nc.sync.dma_start(out=w_raw[h][:], in_=w_view[:, :, h * (N // 2) : (h + 1) * (N // 2)])
+        w_cuts = ((0, 256), (256, 384), (384, 512))
+        w_raw = [sb("w_raw%d" % c0, [P, PACK, c1 - c0], F32) for c0, c1 in w_cuts]
+        for raw, (c0, c1) in zip(w_raw, w_cuts):
+            nc.sync.dma_start(out=raw[:], in_=w_view[:, :, c0:c1])
         for q in range(4):
-            nc.sync.dma_start(
+            (nc.scalar if q < 2 else nc.sync).dma_start(
                 out=x_scale[32 * q : 32 * q + 4, :].bitcast(I32),
                 in_=x_scales[0, 4 * q : 4 * q + 4, :].bitcast(I32),
             )
@@ -59,36 +59,37 @@ def tile_picked_wgrand_none_lo_kernel(
         nc.sync.dma_start(
             out=x_code[:].bitcast(I32), in_=x_words[0].rearrange("p c r -> p (c r)").bitcast(I32)
         )
+        gate_view = gate.rearrange("d p v -> p d v")
+        gates = [sb("gates%d" % h, [P, D - 1, HALF], F32) for h in range(2)]
+        last_gate = sb("last_gate", [P, T], F32)
+        nc.sync.dma_start(out=gates[0][:], in_=gate_view[:, 0 : D - 1, 0:HALF])
+        nc.sync.dma_start(lists[0][:], pos1)
+        nc.sync.dma_start(lists[1][:], pos2)
         nc.sync.dma_start(
             out=gate_rows[0:BLOCKS, :, :], in_=gate[:, 0, :].rearrange("d (b v) -> b d v", v=P)
         )
-        gate_view = gate.rearrange("d p v -> p d v")
-        gates = [sb("gates%d" % h, [P, D, HALF], F32) for h in range(2)]
-        nc.sync.dma_start(lists[0][:], pos1)
-        nc.sync.dma_start(out=gates[0][:], in_=gate_view[:, :, 0:HALF])
-        nc.sync.dma_start(lists[1][:], pos2)
+        nc.sync.dma_start(out=gates[1][:], in_=gate_view[:, 0 : D - 1, HALF:T])
         nc.sync.dma_start(lists[2][:], pos3)
-        nc.sync.dma_start(out=gates[1][:], in_=gate_view[:, :, HALF:T])
+        nc.sync.dma_start(out=last_gate[:], in_=gate[D - 1])
 
-        w_bf = sb("w_bf", [P, PACK, P, PACK], BF16)
-
-        def w_views(h, m0, m1):
-            src = w_raw[h][:, :, PACK * m0 : PACK * m1].rearrange("p j (m t) -> p m t j", t=PACK)
-            dst = w_bf[:, :, 64 * h + m0 : 64 * h + m1, :].rearrange("p t m j -> p m t j")
-            return dst, src
-
-        nc.vector.tensor_copy(*w_views(0, 0, 64))
-        nc.vector.tensor_copy(*w_views(1, 0, W_SPLIT))
-        dst, src = w_views(1, W_SPLIT, 64)
-        nc.scalar.activation(dst, src, COPY)
+        w_bf = [sb("w_bf%d" % u, [P, 2, P, PACK], BF16) for u in range(2)]
+        for raw, (c0, c1) in zip(w_raw, w_cuts):
+            for u in range(2):
+                src = raw[:].rearrange("p j (m t) -> p m t j", t=PACK)[:, :, 2 * u : 2 * u + 2, :]
+                dst = w_bf[u][:, :, c0 // PACK : c1 // PACK, :].rearrange("p t m j -> p m t j")
+                if u == 0:
+                    nc.vector.tensor_copy(dst, src)
+                else:
+                    nc.scalar.activation(dst, src, COPY)
 
         w_code = sb("w_code", [P, N], U32)
         w_scale = sb("w_scale", [P, N], U8)
         for t0, t1 in ((0, 1), (1, 2), (2, 4)):
+            u = t0 // 2
             nc.vector.quantize_mx(
                 out=w_code[:, t0 * P : t1 * P].bitcast(FP8X4),
                 scales=w_scale[:, t0 * P : t1 * P],
-                in_=w_bf[:, t0:t1, :, :].rearrange("p t m j -> p (t m j)"),
+                in_=w_bf[u][:, t0 - 2 * u : t1 - 2 * u, :, :].rearrange("p t m j -> p (t m j)"),
             )
 
         def project(t, c0, c1, acc):
@@ -135,10 +136,9 @@ def tile_picked_wgrand_none_lo_kernel(
                 own[b][:].rearrange("v t p -> v (t p)"), acc[:], COPY, scale=stay[:, b : b + 1]
             )
 
-        def pull(h, t, d):
-            term = sb("term%d_%d_%d" % (h, t, d), [P, HALF], F32)
-            offsets = lists[d][:, h * (HALF // 16) : (h + 1) * (HALF // 16)]
-            nc.vector.tensor_tensor(term[:], y[t][:].indirect(offsets), gates[h][:, d, :], MULT)
+        def pull(term, c0, c1, t, d, factor):
+            offsets = lists[d][:, c0 // 16 : c1 // 16]
+            nc.vector.tensor_tensor(term[:], y[t][:].indirect(offsets), factor, MULT)
             return term
 
         def turn_in(h, t, terms):
@@ -149,73 +149,78 @@ def tile_picked_wgrand_none_lo_kernel(
             nc.scalar.copy(turned[:], acc[:, 0:HALF])
             return turned
 
-        def turn_back(h, t, turned, i):
-            acc = bank(i, "out_acc%d_%d" % (h, t))
+        def turn_back(h, t, turned, acc):
             for b in range(2):
                 turn_add(
                     acc[:, b * P : (b + 1) * P],
                     [own[2 * h + b][:, t, :], turned[:, b * P : (b + 1) * P]],
                 )
-            return acc
 
         out_view = out_0.rearrange("(p t) v -> p t v", t=PACK)
-        result = [sb("result%d" % h, [P, PACK, HALF], F32) for h in range(2)]
-        out_bf = [sb("out_bf%d" % b, [P, P, PACK], BF16) for b in range(BLOCKS)]
+        cuts = ((0, HALF), (HALF, 3 * P), (3 * P, T))
+        result = {c0: sb("result%d" % c0, [P, PACK, c1 - c0], F32) for c0, c1 in cuts}
+        out_bf = {c0: sb("out_bf%d" % c0, [P, c1 - c0, PACK], BF16) for c0, c1 in cuts}
         out_code = sb("out_code", [P, T], U32)
         out_scale = sb("out_scale", [P, T], U8)
         words_view = out_1[0].rearrange("p c r -> p (c r)").bitcast(I32)
 
-        def weave(b, copy):
-            h, c0 = b // 2, (b % 2) * P
-            copy(out_bf[b][:], result[h][:, :, c0 : c0 + P].rearrange("p t v -> p v t"))
-
-        def quantize(b):
+        def quantize(c0, c1):
             nc.vector.quantize_mx(
-                out=out_code[:, b * P : (b + 1) * P].bitcast(FP8X4),
-                scales=out_scale[:, b * P : (b + 1) * P],
-                in_=out_bf[b][:].rearrange("p v t -> p (v t)"),
+                out=out_code[:, c0:c1].bitcast(FP8X4),
+                scales=out_scale[:, c0:c1],
+                in_=out_bf[c0][:].rearrange("p v t -> p (v t)"),
             )
+            nc.sync.dma_start(out=words_view[:, c0:c1], in_=out_code[:, c0:c1].bitcast(I32))
 
-        make_own(0)
-        make_own(1)
-        turned = {}
-        for t in range(PACK + 1):
-            if t < PACK:
-                turned[t] = turn_in(0, t, [pull(0, t, d) for d in range(D)])
-            if t == 1:
-                make_own(2)
-                make_own(3)
-            if t > 0:
-                acc = turn_back(0, t - 1, turned[t - 1], 4 + (t - 1) % 2)
-                nc.scalar.copy(result[0][:, t - 1, :], acc[:, 0:HALF])
-        nc.sync.dma_start(out=out_view[:, :, 0:HALF], in_=result[0][:])
+        steps = [(h, t) for h in range(2) for t in range(PACK)]
+        partial = []
 
-        partial = {}
-        for t in range(PACK + 1):
-            if t < PACK:
-                turned[t] = turn_in(1, t, [pull(1, t, d) for d in range(D - 1)])
-            if t > 0:
-                partial[t - 1] = turn_back(1, t - 1, turned[t - 1], own_banks[t - 1])
-            if t == 1:
-                weave(0, nc.scalar.copy)
-            if t == 2:
-                weave(1, nc.scalar.copy)
-        quantize(0)
-        quantize(1)
-        nc.sync.dma_start(out=words_view[:, 0:HALF], in_=out_code[:, 0:HALF].bitcast(I32))
+        def close(i):
+            h, t = steps[i]
+            if i >= 6:
+                partial.append(bank((7, 0)[i - 6], "single%d" % i)[:, 0:HALF])
+            elif i % 2 == 0:
+                pair = bank(4 + i // 2, "pair%d" % i)
+                partial.extend([pair[:, 0:HALF], pair[:, HALF:T]])
+            turn_back(h, t, turned[i], partial[i])
 
-        last = {}
-        for t in range(PACK + 1):
-            if t < PACK:
-                last[t] = pull(1, t, D - 1)
-            if t > 0:
-                nc.vector.tensor_tensor(result[1][:, t - 1, :], partial[t - 1][:, 0:HALF], last[t - 1][:], ADD)
-                nc.sync.dma_start(out=out_view[:, t - 1, HALF:T], in_=result[1][:, t - 1, :])
-        weave(2, nc.vector.tensor_copy)
-        weave(3, nc.scalar.copy)
-        quantize(2)
-        quantize(3)
-        nc.sync.dma_start(out=words_view[:, HALF:T], in_=out_code[:, HALF:T].bitcast(I32))
+        turned = []
+        for i in range(len(steps) + PACK):
+            if i < len(steps):
+                h, t = steps[i]
+                terms = [
+                    pull(sb("term%d_%d" % (i, d), [P, HALF], F32), h * HALF, (h + 1) * HALF, t, d, gates[h][:, d, :])
+                    for d in range(D - 1)
+                ]
+                turned.append(turn_in(h, t, terms))
+            if i < 2:
+                make_own(2 * i)
+                make_own(2 * i + 1)
+            if i >= PACK:
+                close(i - PACK)
+
+        closing = [(c0, c1, t) for c0, c1 in ((0, HALF), (HALF, 3 * P), (3 * P, T)) for t in range(PACK)]
+        last = []
+        for i in range(len(closing) + 1):
+            if i < len(closing):
+                c0, c1, t = closing[i]
+                term = keep.tile([P, c1 - c0], F32, name="last%d" % i, tag="last", bufs=3, align_bytes=64)
+                last.append(pull(term, c0, c1, t, D - 1, last_gate[:, c0:c1]))
+            if i > 0:
+                c0, c1, t = closing[i - 1]
+                h, r0, r1 = c0 // HALF, c0 % HALF, c0 % HALF + c1 - c0
+                nc.vector.tensor_tensor(
+                    result[c0][:, t, :], partial[PACK * h + t][:, r0:r1], last[i - 1][:], ADD
+                )
+                if t == PACK - 1:
+                    nc.sync.dma_start(out=out_view[:, :, c0:c1], in_=result[c0][:])
+                    copy = nc.vector.tensor_copy if c1 == T else nc.scalar.copy
+                    copy(out_bf[c0][:], result[c0][:].rearrange("p t v -> p v t"))
+            if i == 2 * PACK - 1:
+                quantize(0, HALF)
+            if i == 3 * PACK - 1:
+                quantize(HALF, 3 * P)
+        quantize(3 * P, T)
         for q in range(4):
             queue = nc.scalar if q % 2 else nc.sync
             queue.dma_start(

@@ -38,58 +38,79 @@ def tile_picked_wgrand_none_lo_kernel(
             return psum.tile([P, 512], F32, name=name, tag="bank%d" % i)
 
         lists = [keep.tile([P, T // 16], U16, name="list%d" % d) for d in range(D)]
-        x_scale = sb("x_scale", [P, T], U8)
-        nc.gpsimd.memset(x_scale[:].bitcast(U32), 0)
         gate_rows = sb("gate_rows", [P, D, P], F32)
         nc.gpsimd.memset(gate_rows[:], 0.0)
+        x_scale = sb("x_scale", [P, T], U8)
+        nc.gpsimd.memset(x_scale[:].bitcast(U32), 0)
         ident = sb("ident", [P, P], F32)
         make_identity(nc, ident[:])
 
         w_view = w1.rearrange("(p j) m -> p j m", j=PACK)
-        w_cuts = ((0, 256), (256, 384), (384, 512))
-        w_raw = [sb("w_raw%d" % c0, [P, PACK, c1 - c0], F32) for c0, c1 in w_cuts]
-        for raw, (c0, c1) in zip(w_raw, w_cuts):
-            nc.sync.dma_start(out=raw[:], in_=w_view[:, :, c0:c1])
-        for q in range(4):
-            (nc.scalar if q < 2 else nc.sync).dma_start(
+        w_raw = [sb("w_raw%d" % h, [P, 2, N], F32) for h in range(2)]
+        x_code = sb("x_code", [P, T], U32)
+        gate_view = gate.rearrange("d p v -> p d v")
+        gates = {}
+
+        def load_w(h):
+            nc.sync.dma_start(out=w_raw[h][:], in_=w_view[:, 2 * h : 2 * h + 2, :])
+
+        def load_x():
+            nc.sync.dma_start(
+                out=x_code[:].bitcast(I32), in_=x_words[0].rearrange("p c r -> p (c r)").bitcast(I32)
+            )
+
+        def load_scales(q, queue):
+            queue.dma_start(
                 out=x_scale[32 * q : 32 * q + 4, :].bitcast(I32),
                 in_=x_scales[0, 4 * q : 4 * q + 4, :].bitcast(I32),
             )
-        x_code = sb("x_code", [P, T], U32)
-        nc.sync.dma_start(
-            out=x_code[:].bitcast(I32), in_=x_words[0].rearrange("p c r -> p (c r)").bitcast(I32)
-        )
-        gate_view = gate.rearrange("d p v -> p d v")
-        gates = [sb("gates%d" % h, [P, D - 1, HALF], F32) for h in range(2)]
-        last_gate = sb("last_gate", [P, T], F32)
-        nc.sync.dma_start(out=gates[0][:], in_=gate_view[:, 0 : D - 1, 0:HALF])
-        nc.sync.dma_start(lists[0][:], pos1)
-        nc.sync.dma_start(lists[1][:], pos2)
-        nc.sync.dma_start(
-            out=gate_rows[0:BLOCKS, :, :], in_=gate[:, 0, :].rearrange("d (b v) -> b d v", v=P)
-        )
-        nc.sync.dma_start(out=gates[1][:], in_=gate_view[:, 0 : D - 1, HALF:T])
-        nc.sync.dma_start(lists[2][:], pos3)
-        nc.sync.dma_start(out=last_gate[:], in_=gate[D - 1])
 
-        w_bf = [sb("w_bf%d" % u, [P, 2, P, PACK], BF16) for u in range(2)]
-        for raw, (c0, c1) in zip(w_raw, w_cuts):
-            for u in range(2):
-                src = raw[:].rearrange("p j (m t) -> p m t j", t=PACK)[:, :, 2 * u : 2 * u + 2, :]
-                dst = w_bf[u][:, :, c0 // PACK : c1 // PACK, :].rearrange("p t m j -> p m t j")
-                if u == 0:
+        def load_g(h, d0, d1):
+            rows = sb("gates%d_%d" % (h, d0), [P, d1 - d0, HALF], F32)
+            nc.sync.dma_start(out=rows[:], in_=gate_view[:, d0:d1, h * HALF : (h + 1) * HALF])
+            for d in range(d0, d1):
+                gates[h, d] = rows[:, d - d0, :]
+
+        def load_rows(queue):
+            queue.dma_start(
+                out=gate_rows[0:BLOCKS, :, :], in_=gate[:, 0, :].rearrange("d (b v) -> b d v", v=P)
+            )
+
+        def load_l(d):
+            nc.sync.dma_start(lists[d][:], (pos1, pos2, pos3)[d])
+
+        load_rows(nc.scalar)
+        load_scales(0, nc.scalar)
+        load_scales(1, nc.scalar)
+        load_scales(2, nc.scalar)
+        load_scales(3, nc.scalar)
+        load_w(0)
+        load_w(1)
+        load_x()
+        load_g(0, 0, D)
+        load_l(0)
+        load_l(1)
+        load_l(2)
+        load_g(1, 0, D)
+
+        w_groups = ((0, 1), (1, 2), (2, 4))
+        w_bf = [sb("w_bf%d" % t0, [P, t1 - t0, P, PACK], BF16) for t0, t1 in w_groups]
+        for h in range(2):
+            for (t0, t1), grouped in zip(w_groups, w_bf):
+                src = w_raw[h][:].rearrange("p j (m t) -> p m t j", t=PACK)[:, :, t0:t1, :]
+                dst = grouped[:, :, :, 2 * h : 2 * h + 2].rearrange("p t m j -> p m t j")
+                if t0 < 2:
                     nc.vector.tensor_copy(dst, src)
                 else:
                     nc.scalar.activation(dst, src, COPY)
 
         w_code = sb("w_code", [P, N], U32)
         w_scale = sb("w_scale", [P, N], U8)
-        for t0, t1 in ((0, 1), (1, 2), (2, 4)):
-            u = t0 // 2
+        for (t0, t1), grouped in zip(w_groups, w_bf):
             nc.vector.quantize_mx(
                 out=w_code[:, t0 * P : t1 * P].bitcast(FP8X4),
                 scales=w_scale[:, t0 * P : t1 * P],
-                in_=w_bf[u][:, t0 - 2 * u : t1 - 2 * u, :, :].rearrange("p t m j -> p (t m j)"),
+                in_=grouped[:].rearrange("p t m j -> p (t m j)"),
             )
 
         def project(t, c0, c1, acc):
@@ -103,11 +124,17 @@ def tile_picked_wgrand_none_lo_kernel(
                 stop=True,
             )
 
-        def turn_add(acc, terms):
-            for i, term in enumerate(terms):
-                nc.tensor.matmul(
-                    acc, term, ident[:], start=(i == 0), stop=(i == len(terms) - 1), is_transpose=True
-                )
+        def turn(acc, term, start, stop):
+            nc.tensor.matmul(acc, term, ident[:], start=start, stop=stop, is_transpose=True)
+
+        def block(tile, i):
+            return tile[:, i * P : (i + 1) * P]
+
+        gate_sum = bank(5, "gate_sum")
+        for d in range(D):
+            turn(block(gate_sum, 0), gate_rows[:, d, :], d == 0, d == D - 1)
+        stay = sb("stay", [P, BLOCKS], F32)
+        nc.scalar.activation(stay[:], gate_sum[:, 0:BLOCKS], COPY, bias=1.0, scale=-1.0)
 
         y = [sb("y%d" % t, [P, T], F32) for t in range(PACK)]
         acc_a, acc_b = bank(0, "y0a"), bank(1, "y0b")
@@ -120,46 +147,45 @@ def tile_picked_wgrand_none_lo_kernel(
             project(t, 0, T, acc[:])
             nc.scalar.copy(y[t][:], acc[:])
 
-        gate_sum = bank(5, "gate_sum")
-        turn_add(gate_sum[:, 0:P], [gate_rows[:, d, :] for d in range(D)])
-        stay = sb("stay", [P, BLOCKS], F32)
-        nc.scalar.activation(stay[:], gate_sum[:, 0:BLOCKS], COPY, bias=1.0, scale=-1.0)
-
-        own = [sb("own%d" % b, [P, PACK, P], F32) for b in range(BLOCKS)]
-        own_banks = (6, 7, 0, 1)
+        own = [sb("own%d" % b, [P, T], F32) for b in range(BLOCKS)]
+        own_banks = (5, 6, 7, 0)
+        back_banks = (3, 4, 5, 6)
+        back = []
 
         def make_own(b):
             acc = bank(own_banks[b], "own_acc%d" % b)
             for t in range(PACK):
-                turn_add(acc[:, t * P : (t + 1) * P], [y[t][:, b * P : (b + 1) * P]])
-            nc.scalar.activation(
-                own[b][:].rearrange("v t p -> v (t p)"), acc[:], COPY, scale=stay[:, b : b + 1]
-            )
+                turn(block(acc, t), block(y[t], b), True, True)
+            nc.scalar.activation(own[b][:], acc[:], COPY, scale=stay[:, b : b + 1])
 
-        def pull(term, c0, c1, t, d, factor):
-            offsets = lists[d][:, c0 // 16 : c1 // 16]
-            nc.vector.tensor_tensor(term[:], y[t][:].indirect(offsets), factor, MULT)
-            return term
+        def open_back(b):
+            back.append(bank(back_banks[b], "back%d" % b))
+            for t in range(PACK):
+                turn(block(back[b], t), block(own[b], t), t == 0, False)
 
-        def turn_in(h, t, terms):
-            acc = bank(2 + t % 2, "sum_acc%d_%d" % (h, t))
-            for b in range(2):
-                turn_add(acc[:, b * P : (b + 1) * P], [term[:, b * P : (b + 1) * P] for term in terms])
-            turned = sb("turned%d_%d" % (h, t), [P, HALF], F32)
-            nc.scalar.copy(turned[:], acc[:, 0:HALF])
+        def pull(term, t, d, b0, b1):
+            offsets = lists[d][:, b0 * (P // 16) : b1 * (P // 16)]
+            factor = gates[b0 // 2, d][:, (b0 % 2) * P : (b0 % 2 + b1 - b0) * P]
+            nc.vector.tensor_tensor(term, y[t][:].indirect(offsets), factor, MULT)
+
+        def turn_in(i, t, b0, b1):
+            acc = bank((1, 2, 7, 0)[i % 4] if i > 3 else 1 + i % 2, "sum_acc%d" % i)
+            work = [(d, min(b1, BLOCKS - 1) if d == D - 1 else b1) for d in range(D)]
+            work = [(d, end) for d, end in work if end > b0]
+            for d, end in work:
+                term = sb("term%d_%d" % (i, d), [P, (end - b0) * P], F32)
+                pull(term[:], t, d, b0, end)
+                for b in range(end - b0):
+                    first = d == 0 and b == 0
+                    turn(block(acc, b), block(term, b), first, (d, end) == work[-1] and b == end - b0 - 1)
+            turned = sb("turned%d" % i, [P, (b1 - b0) * P], F32)
+            nc.scalar.copy(turned[:], acc[:, 0 : (b1 - b0) * P])
             return turned
-
-        def turn_back(h, t, turned, acc):
-            for b in range(2):
-                turn_add(
-                    acc[:, b * P : (b + 1) * P],
-                    [own[2 * h + b][:, t, :], turned[:, b * P : (b + 1) * P]],
-                )
 
         out_view = out_0.rearrange("(p t) v -> p t v", t=PACK)
         cuts = ((0, HALF), (HALF, 3 * P), (3 * P, T))
         result = {c0: sb("result%d" % c0, [P, PACK, c1 - c0], F32) for c0, c1 in cuts}
-        out_bf = {c0: sb("out_bf%d" % c0, [P, c1 - c0, PACK], BF16) for c0, c1 in cuts}
+        out_bf = {c0: sb("out_bf%d" % c0, [P, HALF, PACK], BF16) for c0 in (0, HALF)}
         out_code = sb("out_code", [P, T], U32)
         out_scale = sb("out_scale", [P, T], U8)
         words_view = out_1[0].rearrange("p c r -> p (c r)").bitcast(I32)
@@ -172,55 +198,52 @@ def tile_picked_wgrand_none_lo_kernel(
             )
             nc.sync.dma_start(out=words_view[:, c0:c1], in_=out_code[:, c0:c1].bitcast(I32))
 
-        steps = [(h, t) for h in range(2) for t in range(PACK)]
-        partial = []
+        def store(c0, c1):
+            nc.sync.dma_start(out=out_view[:, :, c0:c1], in_=result[c0][:])
 
-        def close(i):
-            h, t = steps[i]
-            if i >= 6:
-                partial.append(bank((7, 0)[i - 6], "single%d" % i)[:, 0:HALF])
-            elif i % 2 == 0:
-                pair = bank(4 + i // 2, "pair%d" % i)
-                partial.extend([pair[:, 0:HALF], pair[:, HALF:T]])
-            turn_back(h, t, turned[i], partial[i])
+        def empty(b):
+            c0 = (b // 2) * HALF
+            cols = slice(b * P - c0, (b + 1) * P - c0)
+            pair = [
+                (result[c0][:, :, cols], back[b][:].rearrange("p (t v) -> p t v", t=PACK)),
+                (out_bf[c0][:, cols, :], back[b][:].rearrange("p (t v) -> p v t", t=PACK)),
+            ]
+            for dst, src in pair:
+                nc.scalar.copy(dst, src)
 
+        steps = [(t, 0, 2) for t in range(PACK)] + [(t, 2, 4) for t in range(PACK - 1)] + [(3, 2, 3), (3, 3, 4)]
         turned = []
-        for i in range(len(steps) + PACK):
+        for b in range(BLOCKS):
+            make_own(b)
+        for i in range(len(steps) + 1):
             if i < len(steps):
-                h, t = steps[i]
-                terms = [
-                    pull(sb("term%d_%d" % (i, d), [P, HALF], F32), h * HALF, (h + 1) * HALF, t, d, gates[h][:, d, :])
-                    for d in range(D - 1)
-                ]
-                turned.append(turn_in(h, t, terms))
-            if i < 2:
-                make_own(2 * i)
-                make_own(2 * i + 1)
-            if i >= PACK:
-                close(i - PACK)
+                turned.append(turn_in(i, *steps[i]))
+            if i == 1:
+                open_back(0)
+                open_back(1)
+            if i == 5:
+                open_back(2)
+                open_back(3)
+            if i >= 1:
+                t, b0, b1 = steps[i - 1]
+                for b in range(b0, b1):
+                    turn(block(back[b], t), block(turned[i - 1], b - b0), False, t == PACK - 1)
+            if i - 1 == 3:
+                empty(0)
+            if i - 1 == 3:
+                empty(1)
+                store(0, HALF)
+        empty(2)
+        store(HALF, 3 * P)
 
-        closing = [(c0, c1, t) for c0, c1 in ((0, HALF), (HALF, 3 * P), (3 * P, T)) for t in range(PACK)]
-        last = []
-        for i in range(len(closing) + 1):
-            if i < len(closing):
-                c0, c1, t = closing[i]
-                term = keep.tile([P, c1 - c0], F32, name="last%d" % i, tag="last", bufs=3, align_bytes=64)
-                last.append(pull(term, c0, c1, t, D - 1, last_gate[:, c0:c1]))
-            if i > 0:
-                c0, c1, t = closing[i - 1]
-                h, r0, r1 = c0 // HALF, c0 % HALF, c0 % HALF + c1 - c0
-                nc.vector.tensor_tensor(
-                    result[c0][:, t, :], partial[PACK * h + t][:, r0:r1], last[i - 1][:], ADD
-                )
-                if t == PACK - 1:
-                    nc.sync.dma_start(out=out_view[:, :, c0:c1], in_=result[c0][:])
-                    copy = nc.vector.tensor_copy if c1 == T else nc.scalar.copy
-                    copy(out_bf[c0][:], result[c0][:].rearrange("p t v -> p v t"))
-            if i == 2 * PACK - 1:
-                quantize(0, HALF)
-            if i == 3 * PACK - 1:
-                quantize(HALF, 3 * P)
-        quantize(3 * P, T)
+        last = sb("last", [P, T], F32)
+        for t in range(PACK):
+            pull(block(last, t), t, D - 1, BLOCKS - 1, BLOCKS)
+        quantize(0, HALF)
+        nc.vector.tensor_tensor(result[3 * P][:].rearrange("p t v -> p (t v)"), back[3][:], last[:], ADD)
+        store(3 * P, T)
+        nc.vector.tensor_copy(out_bf[HALF][:, P:HALF, :], result[3 * P][:].rearrange("p t v -> p v t"))
+        quantize(HALF, T)
         for q in range(4):
             queue = nc.scalar if q % 2 else nc.sync
             queue.dma_start(

@@ -38,12 +38,12 @@ def tile_picked_wgrand_none_lo_kernel(
             return psum.tile([P, 512], F32, name=name, tag="bank%d" % i)
 
         lists = [keep.tile([P, T // 16], U16, name="list%d" % d) for d in range(D)]
-        gate_rows = sb("gate_rows", [P, D, P], F32)
-        nc.gpsimd.memset(gate_rows[:], 0.0)
-        x_scale = sb("x_scale", [P, T], U8)
-        nc.gpsimd.memset(x_scale[:].bitcast(U32), 0)
         ident = sb("ident", [P, P], F32)
         make_identity(nc, ident[:])
+        gate_rows = sb("gate_rows", [P, D, P], F32)
+        nc.vector.memset(gate_rows[:], 0.0)
+        x_scale = sb("x_scale", [P, T], U8)
+        nc.vector.memset(x_scale[:].bitcast(U32), 0)
 
         w_view = w1.rearrange("(p j) m -> p j m", j=PACK)
         w_raw = [sb("w_raw%d" % h, [P, 2, N], F32) for h in range(2)]
@@ -170,7 +170,7 @@ def tile_picked_wgrand_none_lo_kernel(
 
         def turn_in(i, t, b0, b1):
             acc = bank((1, 2, 7, 0)[i % 4] if i > 3 else 1 + i % 2, "sum_acc%d" % i)
-            work = [(d, min(b1, BLOCKS - 1) if d == D - 1 else b1) for d in range(D)]
+            work = [(d, min(b1, BLOCKS - 2) if d == D - 1 else b1) for d in range(D)]
             work = [(d, end) for d, end in work if end > b0]
             for d, end in work:
                 term = sb("term%d_%d" % (i, d), [P, (end - b0) * P], F32)
@@ -183,7 +183,7 @@ def tile_picked_wgrand_none_lo_kernel(
             return turned
 
         out_view = out_0.rearrange("(p t) v -> p t v", t=PACK)
-        cuts = ((0, HALF), (HALF, 3 * P), (3 * P, T))
+        cuts = [(b * P, (b + 1) * P) for b in range(BLOCKS)]
         result = {c0: sb("result%d" % c0, [P, PACK, c1 - c0], F32) for c0, c1 in cuts}
         out_bf = {c0: sb("out_bf%d" % c0, [P, HALF, PACK], BF16) for c0 in (0, HALF)}
         out_code = sb("out_code", [P, T], U32)
@@ -201,17 +201,15 @@ def tile_picked_wgrand_none_lo_kernel(
         def store(c0, c1):
             nc.sync.dma_start(out=out_view[:, :, c0:c1], in_=result[c0][:])
 
-        def empty(b):
-            c0 = (b // 2) * HALF
-            cols = slice(b * P - c0, (b + 1) * P - c0)
-            pair = [
-                (result[c0][:, :, cols], back[b][:].rearrange("p (t v) -> p t v", t=PACK)),
-                (out_bf[c0][:, cols, :], back[b][:].rearrange("p (t v) -> p v t", t=PACK)),
-            ]
-            for dst, src in pair:
-                nc.scalar.copy(dst, src)
+        def woven(b):
+            return out_bf[(b // 2) * HALF][:, (b % 2) * P : (b % 2 + 1) * P, :]
 
-        steps = [(t, 0, 2) for t in range(PACK)] + [(t, 2, 4) for t in range(PACK - 1)] + [(3, 2, 3), (3, 3, 4)]
+        def empty(b):
+            nc.scalar.copy(result[b * P][:], back[b][:].rearrange("p (t v) -> p t v", t=PACK))
+            store(b * P, (b + 1) * P)
+            nc.scalar.copy(woven(b), back[b][:].rearrange("p (t v) -> p v t", t=PACK))
+
+        steps = [(t, 0, 2) for t in range(PACK)] + [(t, 2, 4) for t in range(PACK)]
         turned = []
         for b in range(BLOCKS):
             make_own(b)
@@ -229,20 +227,29 @@ def tile_picked_wgrand_none_lo_kernel(
                 for b in range(b0, b1):
                     turn(block(back[b], t), block(turned[i - 1], b - b0), False, t == PACK - 1)
             if i - 1 == 3:
-                empty(0)
-            if i - 1 == 3:
-                empty(1)
-                store(0, HALF)
-        empty(2)
-        store(HALF, 3 * P)
+                for b in range(BLOCKS - 2):
+                    empty(b)
 
-        last = sb("last", [P, T], F32)
-        for t in range(PACK):
-            pull(block(last, t), t, D - 1, BLOCKS - 1, BLOCKS)
-        quantize(0, HALF)
-        nc.vector.tensor_tensor(result[3 * P][:].rearrange("p t v -> p (t v)"), back[3][:], last[:], ADD)
-        store(3 * P, T)
-        nc.vector.tensor_copy(out_bf[HALF][:, P:HALF, :], result[3 * P][:].rearrange("p t v -> p v t"))
+        last = {}
+
+        def fetch(b):
+            last[b] = keep.tile([P, T], F32, name="last%d" % b, tag="last", bufs=2, align_bytes=64)
+            for t in range(PACK):
+                pull(block(last[b], t), t, D - 1, b, b + 1)
+
+        def close(b):
+            nc.vector.tensor_tensor(result[b * P][:].rearrange("p t v -> p (t v)"), back[b][:], last[b][:], ADD)
+            store(b * P, (b + 1) * P)
+            copy = nc.vector.tensor_copy if b == BLOCKS - 1 else nc.scalar.copy
+            copy(woven(b), result[b * P][:].rearrange("p t v -> p v t"))
+
+        for b in range(BLOCKS - 2, BLOCKS + 1):
+            if b < BLOCKS:
+                fetch(b)
+            if b == BLOCKS:
+                quantize(0, HALF)
+            if b > BLOCKS - 2:
+                close(b - 1)
         quantize(HALF, T)
         for q in range(4):
             queue = nc.scalar if q % 2 else nc.sync

from contextlib import ExitStack

import concourse.mybir as mybir
from concourse.masks import make_identity

K, N, T, D = 512, 512, 512, 3
FLOPS = 2 * K * N * T

F32 = mybir.dt.float32
BF16 = mybir.dt.bfloat16
I32 = mybir.dt.int32
U32 = mybir.dt.uint32
U16 = mybir.dt.uint16
U8 = mybir.dt.uint8
FP8X4 = mybir.dt.float8_e4m3fn_x4
MULT = mybir.AluOpType.mult
ADD = mybir.AluOpType.add
COPY = mybir.ActivationFunctionType.Copy

P = 128
PACK = 4
HALF = T // 2
BLOCKS = T // P


def tile_picked_wgrand_none_lo_kernel(
    tc, x_words, x_scales, w1, gate, pos1, pos2, pos3, out_0, out_1, out_2
):
    nc = tc.nc
    with ExitStack() as ctx:
        keep = ctx.enter_context(tc.tile_pool(name="keep", bufs=1))
        psum = ctx.enter_context(tc.psum_pool(name="psum", bufs=1))

        def sb(name, shape, dtype):
            return keep.tile(shape, dtype, name=name, align_bytes=64)

        def bank(i, name):
            return psum.tile([P, 512], F32, name=name, tag="bank%d" % i)

        lists = [keep.tile([P, T // 16], U16, name="list%d" % d) for d in range(D)]
        ident = sb("ident", [P, P], F32)
        make_identity(nc, ident[:])
        gate_rows = sb("gate_rows", [P, D, P], F32)
        nc.vector.memset(gate_rows[:], 0.0)
        x_scale = sb("x_scale", [P, T], U8)
        nc.vector.memset(x_scale[:].bitcast(U32), 0)

        w_view = w1.rearrange("(p j) m -> p j m", j=PACK)
        w_raw = [sb("w_raw%d" % h, [P, 2, N], F32) for h in range(2)]
        x_code = sb("x_code", [P, T], U32)
        gate_view = gate.rearrange("d p v -> p d v")
        gates = {}

        def load_w(h):
            nc.sync.dma_start(out=w_raw[h][:], in_=w_view[:, 2 * h : 2 * h + 2, :])

        def load_x():
            nc.sync.dma_start(
                out=x_code[:].bitcast(I32), in_=x_words[0].rearrange("p c r -> p (c r)").bitcast(I32)
            )

        def load_scales(q, queue):
            queue.dma_start(
                out=x_scale[32 * q : 32 * q + 4, :].bitcast(I32),
                in_=x_scales[0, 4 * q : 4 * q + 4, :].bitcast(I32),
            )

        def load_g(h, d0, d1):
            rows = sb("gates%d_%d" % (h, d0), [P, d1 - d0, HALF], F32)
            nc.sync.dma_start(out=rows[:], in_=gate_view[:, d0:d1, h * HALF : (h + 1) * HALF])
            for d in range(d0, d1):
                gates[h, d] = rows[:, d - d0, :]

        def load_rows(queue):
            queue.dma_start(
                out=gate_rows[0:BLOCKS, :, :], in_=gate[:, 0, :].rearrange("d (b v) -> b d v", v=P)
            )

        def load_l(d):
            nc.sync.dma_start(lists[d][:], (pos1, pos2, pos3)[d])

        load_rows(nc.scalar)
        load_scales(0, nc.scalar)
        load_scales(1, nc.scalar)
        load_scales(2, nc.scalar)
        load_scales(3, nc.scalar)
        load_w(0)
        load_w(1)
        load_x()
        load_g(0, 0, D)
        load_l(0)
        load_l(1)
        load_l(2)
        load_g(1, 0, D)

        w_groups = ((0, 1), (1, 2), (2, 4))
        w_bf = [sb("w_bf%d" % t0, [P, t1 - t0, P, PACK], BF16) for t0, t1 in w_groups]
        for h in range(2):
            for (t0, t1), grouped in zip(w_groups, w_bf):
                src = w_raw[h][:].rearrange("p j (m t) -> p m t j", t=PACK)[:, :, t0:t1, :]
                dst = grouped[:, :, :, 2 * h : 2 * h + 2].rearrange("p t m j -> p m t j")
                if t0 < 2:
                    nc.vector.tensor_copy(dst, src)
                else:
                    nc.scalar.activation(dst, src, COPY)

        w_code = sb("w_code", [P, N], U32)
        w_scale = sb("w_scale", [P, N], U8)
        for (t0, t1), grouped in zip(w_groups, w_bf):
            nc.vector.quantize_mx(
                out=w_code[:, t0 * P : t1 * P].bitcast(FP8X4),
                scales=w_scale[:, t0 * P : t1 * P],
                in_=grouped[:].rearrange("p t m j -> p (t m j)"),
            )

        def project(t, c0, c1, acc):
            nc.tensor.matmul_mx(
                out=acc,
                lhsT=w_code[:, t * P : (t + 1) * P].bitcast(FP8X4),
                lhsT_scale=w_scale[:, t * P : (t + 1) * P],
                rhs=x_code[:, c0:c1].bitcast(FP8X4),
                rhs_scale=x_scale[:, c0:c1],
                start=True,
                stop=True,
            )

        def turn(acc, term, start, stop):
            nc.tensor.matmul(acc, term, ident[:], start=start, stop=stop, is_transpose=True)

        def block(tile, i):
            return tile[:, i * P : (i + 1) * P]

        gate_sum = bank(5, "gate_sum")
        for d in range(D):
            turn(block(gate_sum, 0), gate_rows[:, d, :], d == 0, d == D - 1)
        stay = sb("stay", [P, BLOCKS], F32)
        nc.scalar.activation(stay[:], gate_sum[:, 0:BLOCKS], COPY, bias=1.0, scale=-1.0)

        y = [sb("y%d" % t, [P, T], F32) for t in range(PACK)]
        acc_a, acc_b = bank(0, "y0a"), bank(1, "y0b")
        project(0, 0, HALF, acc_a[:, 0:HALF])
        project(0, HALF, T, acc_b[:, 0:HALF])
        nc.scalar.copy(y[0][:, 0:HALF], acc_a[:, 0:HALF])
        nc.vector.tensor_copy(y[0][:, HALF:T], acc_b[:, 0:HALF])
        for t in range(1, PACK):
            acc = bank(1 + t, "y_acc%d" % t)
            project(t, 0, T, acc[:])
            nc.scalar.copy(y[t][:], acc[:])

        own = [sb("own%d" % b, [P, T], F32) for b in range(BLOCKS)]
        own_banks = (5, 6, 7, 0)
        back_banks = (3, 4, 5, 6)
        back = []

        def make_own(b):
            acc = bank(own_banks[b], "own_acc%d" % b)
            for t in range(PACK):
                turn(block(acc, t), block(y[t], b), True, True)
            nc.scalar.activation(own[b][:], acc[:], COPY, scale=stay[:, b : b + 1])

        def open_back(b):
            back.append(bank(back_banks[b], "back%d" % b))
            for t in range(PACK):
                turn(block(back[b], t), block(own[b], t), t == 0, False)

        def pull(term, t, d, b0, b1):
            offsets = lists[d][:, b0 * (P // 16) : b1 * (P // 16)]
            factor = gates[b0 // 2, d][:, (b0 % 2) * P : (b0 % 2 + b1 - b0) * P]
            nc.vector.tensor_tensor(term, y[t][:].indirect(offsets), factor, MULT)

        def turn_in(i, t, b0, b1):
            acc = bank((1, 2, 7, 0)[i % 4] if i > 3 else 1 + i % 2, "sum_acc%d" % i)
            work = [(d, min(b1, BLOCKS - 2) if d == D - 1 else b1) for d in range(D)]
            work = [(d, end) for d, end in work if end > b0]
            for d, end in work:
                term = sb("term%d_%d" % (i, d), [P, (end - b0) * P], F32)
                pull(term[:], t, d, b0, end)
                for b in range(end - b0):
                    first = d == 0 and b == 0
                    turn(block(acc, b), block(term, b), first, (d, end) == work[-1] and b == end - b0 - 1)
            turned = sb("turned%d" % i, [P, (b1 - b0) * P], F32)
            nc.scalar.copy(turned[:], acc[:, 0 : (b1 - b0) * P])
            return turned

        out_view = out_0.rearrange("(p t) v -> p t v", t=PACK)
        cuts = [(b * P, (b + 1) * P) for b in range(BLOCKS)]
        result = {c0: sb("result%d" % c0, [P, PACK, c1 - c0], F32) for c0, c1 in cuts}
        out_bf = {c0: sb("out_bf%d" % c0, [P, HALF, PACK], BF16) for c0 in (0, HALF)}
        out_code = sb("out_code", [P, T], U32)
        out_scale = sb("out_scale", [P, T], U8)
        words_view = out_1[0].rearrange("p c r -> p (c r)").bitcast(I32)

        def quantize(c0, c1):
            nc.vector.quantize_mx(
                out=out_code[:, c0:c1].bitcast(FP8X4),
                scales=out_scale[:, c0:c1],
                in_=out_bf[c0][:].rearrange("p v t -> p (v t)"),
            )
            nc.sync.dma_start(out=words_view[:, c0:c1], in_=out_code[:, c0:c1].bitcast(I32))

        def store(c0, c1):
            nc.sync.dma_start(out=out_view[:, :, c0:c1], in_=result[c0][:])

        def woven(b):
            return out_bf[(b // 2) * HALF][:, (b % 2) * P : (b % 2 + 1) * P, :]

        def empty(b):
            nc.scalar.copy(result[b * P][:], back[b][:].rearrange("p (t v) -> p t v", t=PACK))
            store(b * P, (b + 1) * P)
            nc.scalar.copy(woven(b), back[b][:].rearrange("p (t v) -> p v t", t=PACK))

        steps = [(t, 0, 2) for t in range(PACK)] + [(t, 2, 4) for t in range(PACK)]
        turned = []
        for b in range(BLOCKS):
            make_own(b)
        for i in range(len(steps) + 1):
            if i < len(steps):
                turned.append(turn_in(i, *steps[i]))
            if i == 1:
                open_back(0)
                open_back(1)
            if i == 5:
                open_back(2)
                open_back(3)
            if i >= 1:
                t, b0, b1 = steps[i - 1]
                for b in range(b0, b1):
                    turn(block(back[b], t), block(turned[i - 1], b - b0), False, t == PACK - 1)
            if i - 1 == 3:
                for b in range(BLOCKS - 2):
                    empty(b)

        last = {}

        def fetch(b):
            last[b] = keep.tile([P, T], F32, name="last%d" % b, tag="last", bufs=2, align_bytes=64)
            for t in range(PACK):
                pull(block(last[b], t), t, D - 1, b, b + 1)

        def close(b):
            nc.vector.tensor_tensor(result[b * P][:].rearrange("p t v -> p (t v)"), back[b][:], last[b][:], ADD)
            store(b * P, (b + 1) * P)
            copy = nc.vector.tensor_copy if b == BLOCKS - 1 else nc.scalar.copy
            copy(woven(b), result[b * P][:].rearrange("p t v -> p v t"))

        for b in range(BLOCKS - 2, BLOCKS + 1):
            if b < BLOCKS:
                fetch(b)
            if b == BLOCKS:
                quantize(0, HALF)
            if b > BLOCKS - 2:
                close(b - 1)
        quantize(HALF, T)
        for q in range(4):
            queue = nc.scalar if q % 2 else nc.sync
            queue.dma_start(
                out=out_2[0, 4 * q : 4 * q + 4, :].bitcast(I32),
                in_=out_scale[32 * q : 32 * q + 4, :].bitcast(I32),
            )
